import numpy as np
import ml_dtypes


def mxq(x, axis, fmt="e4m3"):
    dtype, down = {"e4m3": (ml_dtypes.float8_e4m3fn, 7), "e5m2": (ml_dtypes.float8_e5m2, 14)}[fmt]
    v = np.moveaxis(np.asarray(x, np.float32).astype(ml_dtypes.bfloat16).astype(np.float64), axis, -1)
    blocks = v.reshape(v.shape[:-1] + (-1, 32))
    amax = np.abs(blocks).max(-1, keepdims=True)
    byte = np.maximum(np.where(amax > 0, np.frexp(amax)[1] - 1 + 127, 0) - down, 1)
    scale = np.exp2(byte - 127.0)
    codes = (blocks / scale).astype(np.float32).astype(dtype).astype(np.float64)
    return np.moveaxis((codes * scale).reshape(v.shape), -1, axis)


WIDE = False


def mx_kscale(k):
    if not WIDE:
        return np.ones(k)
    levels = np.array([10, -10, 5, -5, 0])
    if k % 512:
        return np.exp2(np.random.permutation(np.resize(levels, k // 32))).repeat(32)
    a = np.empty((k // 512, 16))
    for p in range(k // 512):
        a[p, :8] = np.random.permutation(np.resize(levels, 8))
        for g in range(8):
            far = levels[np.abs(levels - a[p, g]) >= 10]
            a[p, g + 8] = far[np.random.randint(len(far))]
    return np.exp2(a.ravel()).repeat(32)


def f64(x):
    return np.asarray(x).astype(np.float64)


def striped(idx):
    return np.tile(idx.reshape(-1, 16).T, (8, 1)).astype(np.uint16)


def unstriped(offs):
    return offs[:16].T.reshape(-1).astype(np.int64)


def pack_weight(w):
    k, n = w.shape
    w = f64(np.asarray(w, np.float32).astype(ml_dtypes.bfloat16)).reshape(k // 32, 32, n)
    amax = np.abs(w).max(1)
    byte = np.clip(np.where(amax > 0, np.frexp(amax)[1] - 1 + 127 - 7, 1), 1, 254)
    scaled = (w * np.exp2(127.0 - byte)[:, None, :]).reshape(k, n).astype(np.float32)
    words = np.ascontiguousarray(scaled.reshape(k // 512, 128, 4, n).transpose(0, 1, 3, 2)).astype(ml_dtypes.float8_e4m3fn).view(np.uint8)
    return words, np.ascontiguousarray(byte.astype(np.uint8).reshape(k // 512, 16, n))


def unpack_weight(words, scales):
    g, p, n, _ = words.shape
    vals = np.ascontiguousarray(words).view(ml_dtypes.float8_e4m3fn).astype(np.float64) * np.repeat(np.exp2(scales.astype(np.float64) - 127.0), 8, axis=1)[..., None]
    return vals.transpose(0, 1, 3, 2).reshape(g * 512, n)


def sigmoid(v):
    return 1.0 / (1.0 + np.exp(-np.maximum(v, -700.0)))


K, T, S, D, N, H, V, U = 512, 2048, 1024, 4, 256, 512, 256, 512


def setup_inputs():
    n = np.random.standard_normal
    s = mx_kscale(K)[:, None]
    u = mx_kscale(H)
    packed_xT = pack_weight(n((K, T)) * s)
    return {
        "x_words": packed_xT[0],
        "x_scales": packed_xT[1],
        "w1": (n((K, H)) / np.sqrt(K) / s).astype(np.float32),
        "w2": (n((K, H)) / np.sqrt(K) / s).astype(np.float32),
        "cost": (np.random.uniform(0.2, 0.9, (H, U))).astype(np.float32),
        "unit": (np.random.uniform(0.6, 1.4, (H, 1)) * u[:, None]).astype(np.float32),
        "w3": (n((H, N)) / np.sqrt(H) / u[:, None]).astype(np.float32),
        "offs": striped(np.random.permutation(T)[:S]),
        "bud": striped(np.random.permutation(np.concatenate([np.arange(V), np.random.randint(0, V, U - V)]))),
    }


def reference(x_words, x_scales, w1, w2, cost, unit, w3, offs, bud):
    xq = unpack_weight(x_words, x_scales)[:, unstriped(offs)]
    en = mxq(f64(w2), 0, "e4m3").T @ xq
    ent = np.log(np.exp(en) + 1.0)
    lg = mxq(f64(w1), 0, "e4m3").T @ xq
    acc_ = np.exp(-1.0 * ent) * sigmoid(lg)
    two = acc_ * (np.pad(acc_, ((0, 0), (0, 1)))[:, 1:])
    gain = two.reshape(len(two), -1, D).sum(axis=2)
    gb = gain[:, unstriped(bud)]
    tree = ent.reshape(len(ent), -1, D).mean(axis=2)
    tb = tree[:, unstriped(bud)]
    hid = f64(unit) * (gb - (f64(cost) * tb))
    return mxq(f64(w3), 0, "e4m3").T @ mxq(hid, 0, "e4m3")

@@ -1,0 +1,204 @@
+from contextlib import ExitStack
+import math
+
+import concourse.mybir as mybir
+
+K, T, S, D, N, H, V, U = 512, 2048, 1024, 4, 256, 512, 256, 512
+FLOPS = 2 * K * H * S * 2 + 2 * H * N * U
+
+F32 = mybir.dt.float32
+BF16 = mybir.dt.bfloat16
+I32 = mybir.dt.int32
+U32 = mybir.dt.uint32
+U16 = mybir.dt.uint16
+U8 = mybir.dt.uint8
+FP8X4 = mybir.dt.float8_e4m3fn_x4
+ACT = mybir.ActivationFunctionType
+ALU = mybir.AluOpType
+
+P = 128
+PACK = 4
+BANK = 512
+HALVES = S // BANK
+VB = BANK // D
+RH = 2
+RW = U // RH
+KNEE = 20.0
+FLOOR = 1.0 / (1.0 + math.exp(KNEE))
+PITCH = V + 8
+
+
+def tile_picked_yentrd_net_p_kernel(tc, x_words, x_scales, w1, w2, cost, unit, w3, offs, bud, out):
+    nc = tc.nc
+    with ExitStack() as ctx:
+        keep = ctx.enter_context(tc.tile_pool(name="keep", bufs=1))
+        psum = ctx.enter_context(tc.psum_pool(name="psum", bufs=8))
+
+        def tile(shape, dtype, name):
+            return keep.tile(shape, dtype, name=name, align_bytes=64)
+
+        offs_sb = tile([P, S // 16], U16, "offs_sb")
+        bud_sb = tile([P, U // 16], U16, "bud_sb")
+        words = tile([P, T], U32, "words")
+        scales = tile([P, T], U8, "scales")
+        w2_raw = tile([P, PACK, H], F32, "w2_raw")
+        w1_raw = tile([P, PACK, H], F32, "w1_raw")
+        w3_raw = tile([P, PACK, N], F32, "w3_raw")
+        cost_sb = tile([P, PACK, U], F32, "cost_sb")
+        unit_sb = tile([P, PACK], F32, "unit_sb")
+
+        nc.gpsimd.memset(scales[:].bitcast(I32), 0)
+        nc.sync.dma_start(offs_sb[:], offs)
+        for q in range(4):
+            nc.sync.dma_start(scales[32 * q : 32 * q + 4, :].bitcast(I32), x_scales[0, 4 * q : 4 * q + 4, :].bitcast(I32))
+        nc.sync.dma_start(words[:].bitcast(I32), x_words[0].rearrange("p n b -> p (n b)").bitcast(I32))
+        nc.sync.dma_start(w2_raw[:], w2.rearrange("(p j) c -> p j c", j=PACK))
+        nc.sync.dma_start(w1_raw[:], w1.rearrange("(p j) c -> p j c", j=PACK))
+        nc.sync.dma_start(bud_sb[:], bud)
+        nc.sync.dma_start(unit_sb[:], unit.rearrange("(p t) o -> p (t o)", t=PACK))
+        nc.sync.dma_start(w3_raw[:], w3.rearrange("(p j) c -> p j c", j=PACK))
+        nc.sync.dma_start(cost_sb[:], cost.rearrange("(p t) r -> p t r", t=PACK))
+
+        acc = [tile([P, D, PITCH], F32, f"acc{t}") for t in range(PACK)]
+        for t in range(PACK):
+            nc.gpsimd.memset(acc[t][:, 0, V:PITCH], 0.0)
+
+        x_sc = [tile([P, BANK], U8, f"x_sc{h}") for h in range(HALVES)]
+        x_cd = [tile([P, BANK], U32, f"x_cd{h}") for h in range(HALVES)]
+        cols = BANK // 16
+        for h in range(HALVES):
+            nc.vector.tensor_copy(x_sc[h][:], scales[:].indirect(offs_sb[:, h * cols : (h + 1) * cols]))
+        for h in range(HALVES):
+            nc.vector.tensor_copy(x_cd[h][:], words[:].indirect(offs_sb[:, h * cols : (h + 1) * cols]))
+
+        def quantise(grouped, name):
+            codes = [tile([P, P], U32, f"{name}_cd{t}") for t in range(PACK)]
+            scl = [tile([P, P], U8, f"{name}_sc{t}") for t in range(PACK)]
+            for t in range(PACK):
+                nc.vector.quantize_mx(out=codes[t][:].bitcast(FP8X4), scales=scl[t][:], in_=grouped[t])
+            return codes, scl
+
+        def product(codes, scl, t, h):
+            bank = psum.tile([P, BANK], F32, name="bank")
+            nc.tensor.matmul_mx(out=bank[:], lhsT=codes[t][:].bitcast(FP8X4), lhsT_scale=scl[t][:],
+                                rhs=x_cd[h][:].bitcast(FP8X4), rhs_scale=x_sc[h][:], start=True, stop=True)
+            return bank[:].rearrange("p (v d) -> p d v", d=D)
+
+        w2_bf = [tile([P, 2, P * PACK], BF16, f"w2_bf{e}") for e in range(2)]
+        w2_src = w2_raw[:].rearrange("p j (m e t) -> p e m j t", e=2, t=2)
+        nc.scalar.copy(w2_bf[0][:].rearrange("p t (m j) -> p m j t", j=PACK), w2_src[:, 0])
+        nc.vector.tensor_copy(w2_bf[1][:].rearrange("p t (m j) -> p m j t", j=PACK), w2_src[:, 1])
+        w2_cd, w2_sc = quantise([w2_bf[t // 2][:, t % 2, :] for t in range(PACK)], "w2")
+
+        w1_bf = [tile([P, P, PACK], BF16, f"w1_bf{t}") for t in range(PACK)]
+        for t in range(PACK):
+            nc.gpsimd.tensor_scalar(w1_bf[t][:], w1_raw[:].rearrange("p j (m t) -> p t m j", t=PACK)[:, t], 1.0, 0.0, ALU.mult, ALU.add)
+
+        keepp = [tile([P, D, V], F32, f"keep{t}") for t in range(PACK)]
+        excess = [tile([P, V], F32, f"excess{t}") for t in range(PACK)]
+        pairs = [tile([P, 2, V], F32, f"pairs{t}") for t in range(PACK)]
+        low = [tile([P, 2, V], F32, f"low{t}") for t in range(PACK)]
+        for t2 in range(0, PACK, 2):
+            en = {}
+            for t in (t2, t2 + 1):
+                for h in range(HALVES):
+                    en[t, h] = product(w2_cd, w2_sc, t, h)
+                    nc.scalar.activation(keepp[t][:, :, h * VB : (h + 1) * VB], en[t, h], ACT.Sigmoid, scale=-1.0)
+                nc.gpsimd.tensor_scalar(low[t][:], keepp[t][:, 0:2, :], 1.0, FLOOR, ALU.min, ALU.max)
+            for d in range(D):
+                for t in (t2, t2 + 1):
+                    for h in range(HALVES):
+                        ex = excess[t][:, h * VB : (h + 1) * VB]
+                        if d == 0:
+                            nc.vector.tensor_scalar(ex, en[t, h][:, d, :], KNEE, D * KNEE, ALU.max, ALU.subtract)
+                        else:
+                            nc.vector.scalar_tensor_tensor(ex, en[t, h][:, d, :], KNEE, ex, ALU.max, ALU.add)
+            if t2 == 0:
+                w1_cd, w1_sc = quantise([w1_bf[t][:].rearrange("p m j -> p (m j)") for t in range(PACK)], "w1")
+        for t in range(PACK):
+            nc.vector.scalar_tensor_tensor(pairs[t][:], keepp[t][:, 2:4, :], FLOOR, low[t][:], ALU.max, ALU.mult)
+
+        like = [tile([P, D, V], F32, f"like{t}") for t in range(PACK)]
+        for t in range(PACK):
+            for h in range(HALVES):
+                lg = product(w1_cd, w1_sc, t, h)
+                nc.scalar.activation(like[t][:, :, h * VB : (h + 1) * VB], lg, ACT.Sigmoid)
+
+        w3_bf = tile([P, N, PACK], BF16, "w3_bf")
+        nc.gpsimd.tensor_scalar(w3_bf[:], w3_raw[:].rearrange("p j c -> p c j"), 1.0, 0.0, ALU.mult, ALU.add)
+
+        tree = [tile([P, 3, V], F32, f"tree{t}") for t in range(PACK)]
+        for t in range(PACK):
+            nc.scalar.activation(tree[t][:, 1:3, :], pairs[t][:], ACT.Ln)
+
+        quarter = tile([P, PACK], F32, "quarter")
+        nc.vector.tensor_scalar(quarter[:], unit_sb[:], 1.0 / D, None, ALU.mult)
+
+        gain = [tile([P, 3, V], F32, f"gain{t}") for t in range(PACK)]
+        gb = [tile([P, PACK, RW], F32, f"gb{r}") for r in range(RH)]
+        tb = [tile([P, PACK, RW], F32, f"tb{r}") for r in range(RH)]
+        spent = [tile([P, PACK, RW], F32, f"spent{r}") for r in range(RH)]
+        bcols = RW // 16
+
+        def window(tl):
+            return tl[:].rearrange("p a v -> p (a v)")
+
+        def make_gain(t):
+            a = acc[t]
+            nc.vector.tensor_tensor(a[:, :, 0:V], keepp[t][:], like[t][:], ALU.mult)
+            side = tile([P, 2, V], F32, f"side{t}")
+            nc.vector.tensor_tensor(side[:, 0, :], a[:, 0, 0:V], a[:, 2, 0:V], ALU.add)
+            nc.vector.tensor_tensor(side[:, 1, :], a[:, 2, 0:V], a[:, 0, 1 : V + 1], ALU.add)
+            nc.vector.scalar_tensor_tensor(gain[t][:, 1:3, :], side[:], unit_sb[:, t : t + 1], a[:, 1:4:2, 0:V], ALU.mult, ALU.mult)
+            nc.vector.tensor_tensor(gain[t][:, 0, :], gain[t][:, 1, :], gain[t][:, 2, :], ALU.add)
+
+        def make_tree(t):
+            part = tile([P, V], F32, f"part{t}")
+            nc.vector.tensor_tensor(part[:], excess[t][:], tree[t][:, 1, :], ALU.subtract)
+            nc.vector.tensor_tensor(tree[t][:, 0, :], part[:], tree[t][:, 2, :], ALU.subtract)
+
+        def fetch(dst, src, t):
+            for r in range(RH):
+                nc.scalar.activation(dst[r][:, t, :], window(src[t]).indirect(bud_sb[:, r * bcols : (r + 1) * bcols]), ACT.Copy)
+
+        make_gain(0)
+        make_gain(1)
+        for t in range(PACK):
+            make_tree(t)
+        fetch(gb, gain, 0)
+        fetch(gb, gain, 1)
+        for t in range(PACK):
+            fetch(tb, tree, t)
+        w3_cd = tile([P, N], U32, "w3_cd")
+        w3_sc = tile([P, N], U8, "w3_sc")
+        nc.vector.quantize_mx(out=w3_cd[:].bitcast(FP8X4), scales=w3_sc[:], in_=w3_bf[:].rearrange("p c j -> p (c j)"))
+        make_gain(2)
+        fetch(gb, gain, 2)
+        make_gain(3)
+        fetch(gb, gain, 3)
+        for r in range(RH):
+            for t in range(PACK):
+                nc.vector.scalar_tensor_tensor(spent[r][:, t, :], tb[r][:, t, :], quarter[:, t : t + 1],
+                                               cost_sb[:, t, r * RW : (r + 1) * RW], ALU.mult, ALU.mult)
+
+        hid = [tile([P, RW, PACK], BF16, f"hid{r}") for r in range(RH)]
+        for r in range(RH):
+            nc.vector.tensor_tensor(hid[r][:].rearrange("p (c i) t -> p c t i", i=4),
+                                    gb[r][:].rearrange("p t (c i) -> p c t i", i=4),
+                                    spent[r][:].rearrange("p t (c i) -> p c t i", i=4), ALU.subtract)
+        for r in range(RH):
+            h_cd = tile([P, RW], U32, f"h_cd{r}")
+            h_sc = tile([P, RW], U8, f"h_sc{r}")
+            nc.vector.quantize_mx(out=h_cd[:].bitcast(FP8X4), scales=h_sc[:], in_=hid[r][:].rearrange("p c t -> p (c t)"))
+            for m in range(N // P):
+                bank = psum.tile([P, BANK], F32, name="bank")
+                nc.tensor.matmul_mx(out=bank[:, 0:RW], lhsT=w3_cd[:, m * P : (m + 1) * P].bitcast(FP8X4),
+                                    lhsT_scale=w3_sc[:, m * P : (m + 1) * P], rhs=h_cd[:].bitcast(FP8X4), rhs_scale=h_sc[:],
+                                    start=True, stop=True)
+                res = tile([P, RW], F32, f"res{r}_{m}")
+                if r == RH - 1 and m == 1:
+                    nc.vector.tensor_copy(res[:], bank[:, 0:RW])
+                else:
+                    nc.scalar.copy(res[:], bank[:, 0:RW])
+                queue = nc.scalar if (r == RH - 1 and m == 0) else nc.sync
+                queue.dma_start(out[m * P : (m + 1) * P, r * RW : (r + 1) * RW], res[:])

@@ -84,15 +84,15 @@ def tile_picked_yentrd_net_p_kernel(tc, x_words, x_scales, w1, w2, cost, unit, w
                                 rhs=x_cd[h][:].bitcast(FP8X4), rhs_scale=x_sc[h][:], start=True, stop=True)
             return bank[:].rearrange("p (v d) -> p d v", d=D)
 
-        w2_bf = [tile([P, 2, P * PACK], BF16, f"w2_bf{e}") for e in range(2)]
-        w2_src = w2_raw[:].rearrange("p j (m e t) -> p e m j t", e=2, t=2)
-        nc.scalar.copy(w2_bf[0][:].rearrange("p t (m j) -> p m j t", j=PACK), w2_src[:, 0])
-        nc.vector.tensor_copy(w2_bf[1][:].rearrange("p t (m j) -> p m j t", j=PACK), w2_src[:, 1])
-        w2_cd, w2_sc = quantise([w2_bf[t // 2][:, t % 2, :] for t in range(PACK)], "w2")
+        def deal(raw, name):
+            grouped = [tile([P, 2, P * PACK], BF16, f"{name}_bf{e}") for e in range(2)]
+            src = raw[:].rearrange("p j (m e t) -> p e m j t", e=2, t=2)
+            nc.scalar.copy(grouped[0][:].rearrange("p t (m j) -> p m j t", j=PACK), src[:, 0])
+            nc.vector.tensor_copy(grouped[1][:].rearrange("p t (m j) -> p m j t", j=PACK), src[:, 1])
+            return [grouped[t // 2][:, t % 2, :] for t in range(PACK)]
 
-        w1_bf = [tile([P, P, PACK], BF16, f"w1_bf{t}") for t in range(PACK)]
-        for t in range(PACK):
-            nc.gpsimd.tensor_scalar(w1_bf[t][:], w1_raw[:].rearrange("p j (m t) -> p t m j", t=PACK)[:, t], 1.0, 0.0, ALU.mult, ALU.add)
+        w2_cd, w2_sc = quantise(deal(w2_raw, "w2"), "w2")
+        w1_bf = deal(w1_raw, "w1")
 
         keepp = [tile([P, D, V], F32, f"keep{t}") for t in range(PACK)]
         excess = [tile([P, V], F32, f"excess{t}") for t in range(PACK)]
@@ -104,7 +104,6 @@ def tile_picked_yentrd_net_p_kernel(tc, x_words, x_scales, w1, w2, cost, unit, w
                 for h in range(HALVES):
                     en[t, h] = product(w2_cd, w2_sc, t, h)
                     nc.scalar.activation(keepp[t][:, :, h * VB : (h + 1) * VB], en[t, h], ACT.Sigmoid, scale=-1.0)
-                nc.gpsimd.tensor_scalar(low[t][:], keepp[t][:, 0:2, :], 1.0, FLOOR, ALU.min, ALU.max)
             for d in range(D):
                 for t in (t2, t2 + 1):
                     for h in range(HALVES):
@@ -114,7 +113,9 @@ def tile_picked_yentrd_net_p_kernel(tc, x_words, x_scales, w1, w2, cost, unit, w
                         else:
                             nc.vector.scalar_tensor_tensor(ex, en[t, h][:, d, :], KNEE, ex, ALU.max, ALU.add)
             if t2 == 0:
-                w1_cd, w1_sc = quantise([w1_bf[t][:].rearrange("p m j -> p (m j)") for t in range(PACK)], "w1")
+                w1_cd, w1_sc = quantise(w1_bf, "w1")
+        for t in range(PACK):
+            nc.vector.tensor_scalar(low[t][:], keepp[t][:, 0:2, :], FLOOR, None, ALU.max)
         for t in range(PACK):
             nc.vector.scalar_tensor_tensor(pairs[t][:], keepp[t][:, 2:4, :], FLOOR, low[t][:], ALU.max, ALU.mult)
 
@@ -124,8 +125,6 @@ def tile_picked_yentrd_net_p_kernel(tc, x_words, x_scales, w1, w2, cost, unit, w
                 lg = product(w1_cd, w1_sc, t, h)
                 nc.scalar.activation(like[t][:, :, h * VB : (h + 1) * VB], lg, ACT.Sigmoid)
 
-        w3_bf = tile([P, N, PACK], BF16, "w3_bf")
-        nc.gpsimd.tensor_scalar(w3_bf[:], w3_raw[:].rearrange("p j c -> p c j"), 1.0, 0.0, ALU.mult, ALU.add)
 
         tree = [tile([P, 3, V], F32, f"tree{t}") for t in range(PACK)]
         for t in range(PACK):
@@ -169,6 +168,8 @@ def tile_picked_yentrd_net_p_kernel(tc, x_words, x_scales, w1, w2, cost, unit, w
         fetch(gb, gain, 1)
         for t in range(PACK):
             fetch(tb, tree, t)
+        w3_bf = tile([P, N, PACK], BF16, "w3_bf")
+        nc.scalar.copy(w3_bf[:].rearrange("p (c i) j -> p c j i", i=4), w3_raw[:].rearrange("p j (c i) -> p c j i", i=4))
         w3_cd = tile([P, N], U32, "w3_cd")
         w3_sc = tile([P, N], U8, "w3_sc")
         nc.vector.quantize_mx(out=w3_cd[:].bitcast(FP8X4), scales=w3_sc[:], in_=w3_bf[:].rearrange("p c j -> p (c j)"))

@@ -47,16 +47,16 @@ def tile_picked_yentrd_net_p_kernel(tc, x_words, x_scales, w1, w2, cost, unit, w
         cost_sb = tile([P, PACK, U], F32, "cost_sb")
         unit_sb = tile([P, PACK], F32, "unit_sb")
 
-        nc.gpsimd.memset(scales[:].bitcast(I32), 0)
         nc.sync.dma_start(offs_sb[:], offs)
         for q in range(4):
-            nc.sync.dma_start(scales[32 * q : 32 * q + 4, :].bitcast(I32), x_scales[0, 4 * q : 4 * q + 4, :].bitcast(I32))
+            rows = x_scales[0, 4 * q : 4 * q + 4, :].bitcast(I32)
+            nc.sync.dma_start(scales[32 * q : 32 * q + 32, :].bitcast(I32), rows.partition_broadcast(8))
         nc.sync.dma_start(words[:].bitcast(I32), x_words[0].rearrange("p n b -> p (n b)").bitcast(I32))
         nc.sync.dma_start(w2_raw[:], w2.rearrange("(p j) c -> p j c", j=PACK))
+        nc.sync.dma_start(w3_raw[:], w3.rearrange("(p j) c -> p j c", j=PACK))
         nc.sync.dma_start(w1_raw[:], w1.rearrange("(p j) c -> p j c", j=PACK))
         nc.sync.dma_start(bud_sb[:], bud)
         nc.sync.dma_start(unit_sb[:], unit.rearrange("(p t) o -> p (t o)", t=PACK))
-        nc.sync.dma_start(w3_raw[:], w3.rearrange("(p j) c -> p j c", j=PACK))
         nc.sync.dma_start(cost_sb[:], cost.rearrange("(p t) r -> p t r", t=PACK))
 
         acc = [tile([P, D, PITCH], F32, f"acc{t}") for t in range(PACK)]
@@ -72,15 +72,16 @@ def tile_picked_yentrd_net_p_kernel(tc, x_words, x_scales, w1, w2, cost, unit, w
             nc.vector.tensor_copy(x_cd[h][:], words[:].indirect(offs_sb[:, h * cols : (h + 1) * cols]))
 
         def quantise(grouped, name):
-            codes = [tile([P, P], U32, f"{name}_cd{t}") for t in range(PACK)]
-            scl = [tile([P, P], U8, f"{name}_sc{t}") for t in range(PACK)]
-            for t in range(PACK):
-                nc.vector.quantize_mx(out=codes[t][:].bitcast(FP8X4), scales=scl[t][:], in_=grouped[t])
+            codes = [tile([P, 2 * P], U32, f"{name}_cd{e}") for e in range(2)]
+            scl = [tile([P, 2 * P], U8, f"{name}_sc{e}") for e in range(2)]
+            for e in range(2):
+                nc.vector.quantize_mx(out=codes[e][:].bitcast(FP8X4), scales=scl[e][:], in_=grouped[e][:].rearrange("p t c -> p (t c)"))
             return codes, scl
 
         def product(codes, scl, t, h):
             bank = psum.tile([P, BANK], F32, name="bank")
-            nc.tensor.matmul_mx(out=bank[:], lhsT=codes[t][:].bitcast(FP8X4), lhsT_scale=scl[t][:],
+            nc.tensor.matmul_mx(out=bank[:], lhsT=codes[t // 2][:, (t % 2) * P : (t % 2 + 1) * P].bitcast(FP8X4),
+                                lhsT_scale=scl[t // 2][:, (t % 2) * P : (t % 2 + 1) * P],
                                 rhs=x_cd[h][:].bitcast(FP8X4), rhs_scale=x_sc[h][:], start=True, stop=True)
             return bank[:].rearrange("p (v d) -> p d v", d=D)
 
@@ -89,9 +90,11 @@ def tile_picked_yentrd_net_p_kernel(tc, x_words, x_scales, w1, w2, cost, unit, w
             src = raw[:].rearrange("p j (m e t) -> p e m j t", e=2, t=2)
             nc.scalar.copy(grouped[0][:].rearrange("p t (m j) -> p m j t", j=PACK), src[:, 0])
             nc.vector.tensor_copy(grouped[1][:].rearrange("p t (m j) -> p m j t", j=PACK), src[:, 1])
-            return [grouped[t // 2][:, t % 2, :] for t in range(PACK)]
+            return grouped
 
         w2_cd, w2_sc = quantise(deal(w2_raw, "w2"), "w2")
+        w3_bf = tile([P, N, PACK], BF16, "w3_bf")
+        nc.scalar.copy(w3_bf[:].rearrange("p (c i) j -> p c j i", i=4), w3_raw[:].rearrange("p j (c i) -> p c j i", i=4))
         w1_bf = deal(w1_raw, "w1")
 
         keepp = [tile([P, D, V], F32, f"keep{t}") for t in range(PACK)]
@@ -135,71 +138,76 @@ def tile_picked_yentrd_net_p_kernel(tc, x_words, x_scales, w1, w2, cost, unit, w
 
         gain = [tile([P, 3, V], F32, f"gain{t}") for t in range(PACK)]
         gb = [tile([P, PACK, RW], F32, f"gb{r}") for r in range(RH)]
-        tb = [tile([P, PACK, RW], F32, f"tb{r}") for r in range(RH)]
-        spent = [tile([P, PACK, RW], F32, f"spent{r}") for r in range(RH)]
+        tb = [tile([P, U], F32, f"tb{t}") for t in range(PACK)]
+
         bcols = RW // 16
 
         def window(tl):
             return tl[:].rearrange("p a v -> p (a v)")
 
-        def make_gain(t):
-            a = acc[t]
-            nc.vector.tensor_tensor(a[:, :, 0:V], keepp[t][:], like[t][:], ALU.mult)
-            side = tile([P, 2, V], F32, f"side{t}")
-            nc.vector.tensor_tensor(side[:, 0, :], a[:, 0, 0:V], a[:, 2, 0:V], ALU.add)
-            nc.vector.tensor_tensor(side[:, 1, :], a[:, 2, 0:V], a[:, 0, 1 : V + 1], ALU.add)
-            nc.vector.scalar_tensor_tensor(gain[t][:, 1:3, :], side[:], unit_sb[:, t : t + 1], a[:, 1:4:2, 0:V], ALU.mult, ALU.mult)
-            nc.vector.tensor_tensor(gain[t][:, 0, :], gain[t][:, 1, :], gain[t][:, 2, :], ALU.add)
+        def make_gain(tiles):
+            both = keep.tile([P, 2, 2, V], F32, name=f"side{tiles[0]}", tag=f"shared{tiles[0]}", align_bytes=64)
+            side = {t: both[:, t % 2] for t in tiles}
+            for t in tiles:
+                nc.vector.tensor_tensor(acc[t][:, :, 0:V], keepp[t][:], like[t][:], ALU.mult)
+            for t in tiles:
+                nc.vector.tensor_tensor(side[t][:, 0, :], acc[t][:, 0, 0:V], acc[t][:, 2, 0:V], ALU.add)
+            for t in tiles:
+                nc.vector.tensor_tensor(side[t][:, 1, :], acc[t][:, 2, 0:V], acc[t][:, 0, 1 : V + 1], ALU.add)
+            for t in tiles:
+                nc.vector.scalar_tensor_tensor(gain[t][:, 1:3, :], side[t], unit_sb[:, t : t + 1], acc[t][:, 1:4:2, 0:V], ALU.mult, ALU.mult)
+            for t in tiles:
+                nc.vector.tensor_tensor(gain[t][:, 0, :], gain[t][:, 1, :], gain[t][:, 2, :], ALU.add)
 
-        def make_tree(t):
-            part = tile([P, V], F32, f"part{t}")
-            nc.vector.tensor_tensor(part[:], excess[t][:], tree[t][:, 1, :], ALU.subtract)
-            nc.vector.tensor_tensor(tree[t][:, 0, :], part[:], tree[t][:, 2, :], ALU.subtract)
-
-        def fetch(dst, src, t):
+        def fetch(dst, src, tiles):
             for r in range(RH):
-                nc.scalar.activation(dst[r][:, t, :], window(src[t]).indirect(bud_sb[:, r * bcols : (r + 1) * bcols]), ACT.Copy)
+                for t in tiles:
+                    nc.scalar.activation(dst[r][:, t, :], window(src[t]).indirect(bud_sb[:, r * bcols : (r + 1) * bcols]), ACT.Copy)
 
-        make_gain(0)
-        make_gain(1)
+        make_gain((0, 1))
+        part = [tile([P, V], F32, f"part{t}") for t in range(PACK)]
         for t in range(PACK):
-            make_tree(t)
-        fetch(gb, gain, 0)
-        fetch(gb, gain, 1)
+            nc.vector.tensor_tensor(part[t][:], excess[t][:], tree[t][:, 1, :], ALU.subtract)
         for t in range(PACK):
-            fetch(tb, tree, t)
-        w3_bf = tile([P, N, PACK], BF16, "w3_bf")
-        nc.scalar.copy(w3_bf[:].rearrange("p (c i) j -> p c j i", i=4), w3_raw[:].rearrange("p j (c i) -> p c j i", i=4))
+            nc.vector.tensor_tensor(tree[t][:, 0, :], part[t][:], tree[t][:, 2, :], ALU.subtract)
+        fetch(gb, gain, (0, 1))
+        for t in range(PACK):
+            nc.scalar.activation(tb[t][:], window(tree[t]).indirect(bud_sb[:]), ACT.Copy)
         w3_cd = tile([P, N], U32, "w3_cd")
         w3_sc = tile([P, N], U8, "w3_sc")
         nc.vector.quantize_mx(out=w3_cd[:].bitcast(FP8X4), scales=w3_sc[:], in_=w3_bf[:].rearrange("p c j -> p (c j)"))
-        make_gain(2)
-        fetch(gb, gain, 2)
-        make_gain(3)
-        fetch(gb, gain, 3)
-        for r in range(RH):
-            for t in range(PACK):
-                nc.vector.scalar_tensor_tensor(spent[r][:, t, :], tb[r][:, t, :], quarter[:, t : t + 1],
-                                               cost_sb[:, t, r * RW : (r + 1) * RW], ALU.mult, ALU.mult)
+        make_gain((2, 3))
+        fetch(gb, gain, (2, 3))
+        spent = keep.tile([P, PACK, U], F32, name="spent", tag="shared2", align_bytes=64)
+        for t in range(PACK):
+            nc.vector.scalar_tensor_tensor(spent[:, t, :], tb[t][:], quarter[:, t : t + 1], cost_sb[:, t, :], ALU.mult, ALU.mult)
 
-        hid = [tile([P, RW, PACK], BF16, f"hid{r}") for r in range(RH)]
-        for r in range(RH):
-            nc.vector.tensor_tensor(hid[r][:].rearrange("p (c i) t -> p c t i", i=4),
-                                    gb[r][:].rearrange("p t (c i) -> p c t i", i=4),
-                                    spent[r][:].rearrange("p t (c i) -> p c t i", i=4), ALU.subtract)
-        for r in range(RH):
-            h_cd = tile([P, RW], U32, f"h_cd{r}")
-            h_sc = tile([P, RW], U8, f"h_sc{r}")
-            nc.vector.quantize_mx(out=h_cd[:].bitcast(FP8X4), scales=h_sc[:], in_=hid[r][:].rearrange("p c t -> p (c t)"))
+        CW = 128
+        pieces = U // CW
+        per = RW // CW
+        hid = [tile([P, CW, PACK], BF16, f"hid{c}") for c in range(pieces)]
+
+        def subtract(c):
+            cols_c = slice((c % per) * CW, (c % per + 1) * CW)
+            nc.vector.tensor_tensor(hid[c][:].rearrange("p (c i) t -> p c t i", i=4),
+                                    gb[c // per][:, :, cols_c].rearrange("p t (c i) -> p c t i", i=4),
+                                    spent[:, :, c * CW : (c + 1) * CW].rearrange("p t (c i) -> p c t i", i=4), ALU.subtract)
+
+        def finish(c):
+            h_cd = tile([P, CW], U32, f"h_cd{c}")
+            h_sc = tile([P, CW], U8, f"h_sc{c}")
+            nc.vector.quantize_mx(out=h_cd[:].bitcast(FP8X4), scales=h_sc[:], in_=hid[c][:].rearrange("p c t -> p (c t)"))
+            bank = psum.tile([P, BANK], F32, name="bank")
             for m in range(N // P):
-                bank = psum.tile([P, BANK], F32, name="bank")
-                nc.tensor.matmul_mx(out=bank[:, 0:RW], lhsT=w3_cd[:, m * P : (m + 1) * P].bitcast(FP8X4),
+                nc.tensor.matmul_mx(out=bank[:, m * CW : (m + 1) * CW], lhsT=w3_cd[:, m * P : (m + 1) * P].bitcast(FP8X4),
                                     lhsT_scale=w3_sc[:, m * P : (m + 1) * P], rhs=h_cd[:].bitcast(FP8X4), rhs_scale=h_sc[:],
                                     start=True, stop=True)
-                res = tile([P, RW], F32, f"res{r}_{m}")
-                if r == RH - 1 and m == 1:
-                    nc.vector.tensor_copy(res[:], bank[:, 0:RW])
-                else:
-                    nc.scalar.copy(res[:], bank[:, 0:RW])
-                queue = nc.scalar if (r == RH - 1 and m == 0) else nc.sync
-                queue.dma_start(out[m * P : (m + 1) * P, r * RW : (r + 1) * RW], res[:])
+            res = tile([P, N // P, CW], F32, f"res{c}")
+            nc.scalar.copy(res[:].rearrange("p m c -> p (m c)"), bank[:, 0 : (N // P) * CW])
+            nc.sync.dma_start(out[:, c * CW : (c + 1) * CW].rearrange("(m p) c -> p m c", p=P), res[:])
+
+        subtract(0)
+        for c in range(1, pieces):
+            subtract(c)
+            finish(c - 1)
+        finish(pieces - 1)

@@ -23,8 +23,8 @@ HALVES = S // BANK
 VB = BANK // D
 RH = 2
 RW = U // RH
-KNEE = 20.0
-FLOOR = 1.0 / (1.0 + math.exp(KNEE))
+KNEE = 12.25
+LIFT = 256.0
 PITCH = V + 8
 
 
@@ -59,6 +59,10 @@ def tile_picked_yentrd_net_p_kernel(tc, x_words, x_scales, w1, w2, cost, unit, w
         nc.sync.dma_start(unit_sb[:], unit.rearrange("(p t) o -> p (t o)", t=PACK))
         nc.sync.dma_start(cost_sb[:], cost.rearrange("(p t) r -> p t r", t=PACK))
 
+        knee = tile([P, 1], F32, "knee")
+        nc.gpsimd.memset(knee[:], KNEE)
+        floor = tile([P, 1], F32, "floor")
+        nc.scalar.activation(floor[:], knee[:], ACT.Sigmoid, scale=-1.0)
         acc = [tile([P, D, PITCH], F32, f"acc{t}") for t in range(PACK)]
         for t in range(PACK):
             nc.gpsimd.memset(acc[t][:, 0, V:PITCH], 0.0)
@@ -71,67 +75,60 @@ def tile_picked_yentrd_net_p_kernel(tc, x_words, x_scales, w1, w2, cost, unit, w
         for h in range(HALVES):
             nc.vector.tensor_copy(x_cd[h][:], words[:].indirect(offs_sb[:, h * cols : (h + 1) * cols]))
 
-        def quantise(grouped, name):
-            codes = [tile([P, 2 * P], U32, f"{name}_cd{e}") for e in range(2)]
-            scl = [tile([P, 2 * P], U8, f"{name}_sc{e}") for e in range(2)]
-            for e in range(2):
-                nc.vector.quantize_mx(out=codes[e][:].bitcast(FP8X4), scales=scl[e][:], in_=grouped[e][:].rearrange("p t c -> p (t c)"))
-            return codes, scl
-
-        def product(codes, scl, t, h):
+        def product(weights, t, h):
+            codes, scl = weights[t // 2]
             bank = psum.tile([P, BANK], F32, name="bank")
-            nc.tensor.matmul_mx(out=bank[:], lhsT=codes[t // 2][:, (t % 2) * P : (t % 2 + 1) * P].bitcast(FP8X4),
-                                lhsT_scale=scl[t // 2][:, (t % 2) * P : (t % 2 + 1) * P],
+            nc.tensor.matmul_mx(out=bank[:], lhsT=codes[:, (t % 2) * P : (t % 2 + 1) * P].bitcast(FP8X4),
+                                lhsT_scale=scl[:, (t % 2) * P : (t % 2 + 1) * P],
                                 rhs=x_cd[h][:].bitcast(FP8X4), rhs_scale=x_sc[h][:], start=True, stop=True)
             return bank[:].rearrange("p (v d) -> p d v", d=D)
 
-        def deal(raw, name):
-            grouped = [tile([P, 2, P * PACK], BF16, f"{name}_bf{e}") for e in range(2)]
+        def deal(raw, name, e, move):
+            grouped = tile([P, 2, P * PACK], BF16, f"{name}_bf{e}")
             src = raw[:].rearrange("p j (m e t) -> p e m j t", e=2, t=2)
-            nc.scalar.copy(grouped[0][:].rearrange("p t (m j) -> p m j t", j=PACK), src[:, 0])
-            nc.vector.tensor_copy(grouped[1][:].rearrange("p t (m j) -> p m j t", j=PACK), src[:, 1])
-            return grouped
+            move(grouped[:].rearrange("p t (m j) -> p m j t", j=PACK), src[:, e])
+            codes = tile([P, 2 * P], U32, f"{name}_cd{e}")
+            scl = tile([P, 2 * P], U8, f"{name}_sc{e}")
+            nc.vector.quantize_mx(out=codes[:].bitcast(FP8X4), scales=scl[:], in_=grouped[:].rearrange("p t c -> p (t c)"))
+            return codes, scl
 
-        w2_cd, w2_sc = quantise(deal(w2_raw, "w2"), "w2")
-        w3_bf = tile([P, N, PACK], BF16, "w3_bf")
-        nc.scalar.copy(w3_bf[:].rearrange("p (c i) j -> p c j i", i=4), w3_raw[:].rearrange("p j (c i) -> p c j i", i=4))
-        w1_bf = deal(w1_raw, "w1")
+        w2_q = [deal(w2_raw, "w2", 0, nc.vector.tensor_copy), deal(w2_raw, "w2", 1, nc.scalar.copy)]
 
-        keepp = [tile([P, D, V], F32, f"keep{t}") for t in range(PACK)]
-        excess = [tile([P, V], F32, f"excess{t}") for t in range(PACK)]
-        pairs = [tile([P, 2, V], F32, f"pairs{t}") for t in range(PACK)]
-        low = [tile([P, 2, V], F32, f"low{t}") for t in range(PACK)]
+        keep2 = [tile([P, 2, D, V], F32, f"keep{e}") for e in range(2)]
+        keepp = [keep2[t // 2][:, t % 2] for t in range(PACK)]
+        tree = [tile([P, 3, V], F32, f"tree{t}") for t in range(PACK)]
+        prod = [tile([P, 2, V], F32, f"prod{e}") for e in range(2)]
+        en = {}
+        for t in range(PACK):
+            for h in range(HALVES):
+                en[t, h] = product(w2_q, t, h)
+                nc.scalar.activation(keepp[t][:, :, h * VB : (h + 1) * VB], en[t, h], ACT.Sigmoid, scale=-1.0)
+        w1_q = [deal(w1_raw, "w1", 0, nc.vector.tensor_copy), deal(w1_raw, "w1", 1, nc.scalar.copy)]
         for t2 in range(0, PACK, 2):
-            en = {}
-            for t in (t2, t2 + 1):
-                for h in range(HALVES):
-                    en[t, h] = product(w2_cd, w2_sc, t, h)
-                    nc.scalar.activation(keepp[t][:, :, h * VB : (h + 1) * VB], en[t, h], ACT.Sigmoid, scale=-1.0)
             for d in range(D):
                 for t in (t2, t2 + 1):
                     for h in range(HALVES):
-                        ex = excess[t][:, h * VB : (h + 1) * VB]
+                        ex = tree[t][:, 2, h * VB : (h + 1) * VB]
                         if d == 0:
                             nc.vector.tensor_scalar(ex, en[t, h][:, d, :], KNEE, D * KNEE, ALU.max, ALU.subtract)
                         else:
                             nc.vector.scalar_tensor_tensor(ex, en[t, h][:, d, :], KNEE, ex, ALU.max, ALU.add)
-            if t2 == 0:
-                w1_cd, w1_sc = quantise(w1_bf, "w1")
-        for t in range(PACK):
-            nc.vector.tensor_scalar(low[t][:], keepp[t][:, 0:2, :], FLOOR, None, ALU.max)
-        for t in range(PACK):
-            nc.vector.scalar_tensor_tensor(pairs[t][:], keepp[t][:, 2:4, :], FLOOR, low[t][:], ALU.max, ALU.mult)
+        for d in range(D):
+            for e in range(2):
+                if d == 0:
+                    nc.vector.tensor_scalar(prod[e][:], keep2[e][:, :, d, :], floor[:], None, ALU.max)
+                else:
+                    nc.vector.scalar_tensor_tensor(prod[e][:], keep2[e][:, :, d, :], floor[:], prod[e][:], ALU.max, ALU.mult)
 
         like = [tile([P, D, V], F32, f"like{t}") for t in range(PACK)]
         for t in range(PACK):
             for h in range(HALVES):
-                lg = product(w1_cd, w1_sc, t, h)
+                lg = product(w1_q, t, h)
                 nc.scalar.activation(like[t][:, :, h * VB : (h + 1) * VB], lg, ACT.Sigmoid)
 
 
-        tree = [tile([P, 3, V], F32, f"tree{t}") for t in range(PACK)]
         for t in range(PACK):
-            nc.scalar.activation(tree[t][:, 1:3, :], pairs[t][:], ACT.Ln)
+            nc.scalar.activation(tree[t][:, 1, :], prod[t // 2][:, t % 2, :], ACT.Ln, scale=LIFT)
 
         quarter = tile([P, PACK], F32, "quarter")
         nc.vector.tensor_scalar(quarter[:], unit_sb[:], 1.0 / D, None, ALU.mult)
@@ -149,7 +146,7 @@ def tile_picked_yentrd_net_p_kernel(tc, x_words, x_scales, w1, w2, cost, unit, w
             both = keep.tile([P, 2, 2, V], F32, name=f"side{tiles[0]}", tag=f"shared{tiles[0]}", align_bytes=64)
             side = {t: both[:, t % 2] for t in tiles}
             for t in tiles:
-                nc.vector.tensor_tensor(acc[t][:, :, 0:V], keepp[t][:], like[t][:], ALU.mult)
+                nc.vector.tensor_tensor(acc[t][:, :, 0:V], keepp[t], like[t][:], ALU.mult)
             for t in tiles:
                 nc.vector.tensor_tensor(side[t][:, 0, :], acc[t][:, 0, 0:V], acc[t][:, 2, 0:V], ALU.add)
             for t in tiles:
@@ -164,15 +161,14 @@ def tile_picked_yentrd_net_p_kernel(tc, x_words, x_scales, w1, w2, cost, unit, w
                 for t in tiles:
                     nc.scalar.activation(dst[r][:, t, :], window(src[t]).indirect(bud_sb[:, r * bcols : (r + 1) * bcols]), ACT.Copy)
 
-        make_gain((0, 1))
-        part = [tile([P, V], F32, f"part{t}") for t in range(PACK)]
         for t in range(PACK):
-            nc.vector.tensor_tensor(part[t][:], excess[t][:], tree[t][:, 1, :], ALU.subtract)
-        for t in range(PACK):
-            nc.vector.tensor_tensor(tree[t][:, 0, :], part[t][:], tree[t][:, 2, :], ALU.subtract)
-        fetch(gb, gain, (0, 1))
+            nc.vector.scalar_tensor_tensor(tree[t][:, 0, :], tree[t][:, 2, :], math.log(LIFT), tree[t][:, 1, :], ALU.add, ALU.subtract)
         for t in range(PACK):
             nc.scalar.activation(tb[t][:], window(tree[t]).indirect(bud_sb[:]), ACT.Copy)
+        make_gain((0, 1))
+        fetch(gb, gain, (0, 1))
+        w3_bf = tile([P, N, PACK], BF16, "w3_bf")
+        nc.scalar.copy(w3_bf[:], w3_raw[:].rearrange("p j c -> p c j"))
         w3_cd = tile([P, N], U32, "w3_cd")
         w3_sc = tile([P, N], U8, "w3_sc")
         nc.vector.quantize_mx(out=w3_cd[:].bitcast(FP8X4), scales=w3_sc[:], in_=w3_bf[:].rearrange("p c j -> p (c j)"))
@@ -187,11 +183,15 @@ def tile_picked_yentrd_net_p_kernel(tc, x_words, x_scales, w1, w2, cost, unit, w
         per = RW // CW
         hid = [tile([P, CW, PACK], BF16, f"hid{c}") for c in range(pieces)]
 
+        flat = [tile([P, PACK, CW], BF16, f"flat{c}") for c in range(pieces)]
+
         def subtract(c):
             cols_c = slice((c % per) * CW, (c % per + 1) * CW)
-            nc.vector.tensor_tensor(hid[c][:].rearrange("p (c i) t -> p c t i", i=4),
-                                    gb[c // per][:, :, cols_c].rearrange("p t (c i) -> p c t i", i=4),
-                                    spent[:, :, c * CW : (c + 1) * CW].rearrange("p t (c i) -> p c t i", i=4), ALU.subtract)
+            nc.vector.tensor_tensor(flat[c][:], gb[c // per][:, :, cols_c], spent[:, :, c * CW : (c + 1) * CW], ALU.subtract)
+
+        def weave(c):
+            move = nc.vector.tensor_copy if c == pieces - 1 else nc.scalar.copy
+            move(hid[c][:], flat[c][:].rearrange("p t c -> p c t"))
 
         def finish(c):
             h_cd = tile([P, CW], U32, f"h_cd{c}")
@@ -206,8 +206,10 @@ def tile_picked_yentrd_net_p_kernel(tc, x_words, x_scales, w1, w2, cost, unit, w
             nc.scalar.copy(res[:].rearrange("p m c -> p (m c)"), bank[:, 0 : (N // P) * CW])
             nc.sync.dma_start(out[:, c * CW : (c + 1) * CW].rearrange("(m p) c -> p m c", p=P), res[:])
 
-        subtract(0)
-        for c in range(1, pieces):
-            subtract(c)
-            finish(c - 1)
-        finish(pieces - 1)
+        for step in range(pieces + 2):
+            if step < pieces:
+                subtract(step)
+            if 1 <= step <= pieces:
+                weave(step - 1)
+            if step >= 2:
+                finish(step - 2)

@@ -18,27 +18,28 @@ ALU = mybir.AluOpType
 
 P = 128
 PACK = 4
+PER_COLUMN = 16
 BANK = 512
 HALVES = S // BANK
-VB = BANK // D
-RH = 2
-RW = U // RH
+BANK_BRANCHES = BANK // D
+PITCH = V + 8
 KNEE = 12.25
 LIFT = 256.0
-PITCH = V + 8
+GAIN_WIDTH = 256
+PIECE = 128
 
 
 def tile_picked_yentrd_net_p_kernel(tc, x_words, x_scales, w1, w2, cost, unit, w3, offs, bud, out):
     nc = tc.nc
     with ExitStack() as ctx:
-        keep = ctx.enter_context(tc.tile_pool(name="keep", bufs=1))
+        sbuf = ctx.enter_context(tc.tile_pool(name="sbuf", bufs=1))
         psum = ctx.enter_context(tc.psum_pool(name="psum", bufs=8))
 
         def tile(shape, dtype, name):
-            return keep.tile(shape, dtype, name=name, align_bytes=64)
+            return sbuf.tile(shape, dtype, name=name, align_bytes=64)
 
-        offs_sb = tile([P, S // 16], U16, "offs_sb")
-        bud_sb = tile([P, U // 16], U16, "bud_sb")
+        offs_sb = tile([P, S // PER_COLUMN], U16, "offs_sb")
+        bud_sb = tile([P, U // PER_COLUMN], U16, "bud_sb")
         words = tile([P, T], U32, "words")
         scales = tile([P, T], U8, "scales")
         w2_raw = tile([P, PACK, H], F32, "w2_raw")
@@ -65,151 +66,159 @@ def tile_picked_yentrd_net_p_kernel(tc, x_words, x_scales, w1, w2, cost, unit, w
         nc.scalar.activation(floor[:], knee[:], ACT.Sigmoid, scale=-1.0)
         acc = [tile([P, D, PITCH], F32, f"acc{t}") for t in range(PACK)]
         for t in range(PACK):
-            nc.gpsimd.memset(acc[t][:, 0, V:PITCH], 0.0)
+            nc.gpsimd.memset(acc[t][:, 0, V : V + 1], 0.0)
 
-        x_sc = [tile([P, BANK], U8, f"x_sc{h}") for h in range(HALVES)]
-        x_cd = [tile([P, BANK], U32, f"x_cd{h}") for h in range(HALVES)]
-        cols = BANK // 16
+        picked_scales = [tile([P, BANK], U8, f"picked_scales{h}") for h in range(HALVES)]
+        picked_words = [tile([P, BANK], U32, f"picked_words{h}") for h in range(HALVES)]
+        offs_half = [offs_sb[:, h * BANK // PER_COLUMN : (h + 1) * BANK // PER_COLUMN] for h in range(HALVES)]
         for h in range(HALVES):
-            nc.vector.tensor_copy(x_sc[h][:], scales[:].indirect(offs_sb[:, h * cols : (h + 1) * cols]))
+            nc.vector.tensor_copy(picked_scales[h][:], scales[:].indirect(offs_half[h]))
         for h in range(HALVES):
-            nc.vector.tensor_copy(x_cd[h][:], words[:].indirect(offs_sb[:, h * cols : (h + 1) * cols]))
+            nc.vector.tensor_copy(picked_words[h][:], words[:].indirect(offs_half[h]))
+
+        def quantise_pair(raw, name, e, copy):
+            rounded = tile([P, 2, P * PACK], BF16, f"{name}_rounded{e}")
+            source = raw[:].rearrange("p j (m e s) -> p e m j s", e=2, s=2)
+            copy(rounded[:].rearrange("p s (m j) -> p m j s", j=PACK), source[:, e])
+            codes = tile([P, 2 * P], U32, f"{name}_codes{e}")
+            code_scales = tile([P, 2 * P], U8, f"{name}_scales{e}")
+            nc.vector.quantize_mx(out=codes[:].bitcast(FP8X4), scales=code_scales[:], in_=rounded[:].rearrange("p s c -> p (s c)"))
+            return codes, code_scales
+
+        def quantise_weights(raw, name):
+            return [quantise_pair(raw, name, 0, nc.vector.tensor_copy), quantise_pair(raw, name, 1, nc.scalar.copy)]
 
         def product(weights, t, h):
-            codes, scl = weights[t // 2]
+            codes, code_scales = weights[t // 2]
+            columns = slice((t % 2) * P, (t % 2 + 1) * P)
             bank = psum.tile([P, BANK], F32, name="bank")
-            nc.tensor.matmul_mx(out=bank[:], lhsT=codes[:, (t % 2) * P : (t % 2 + 1) * P].bitcast(FP8X4),
-                                lhsT_scale=scl[:, (t % 2) * P : (t % 2 + 1) * P],
-                                rhs=x_cd[h][:].bitcast(FP8X4), rhs_scale=x_sc[h][:], start=True, stop=True)
+            nc.tensor.matmul_mx(out=bank[:], lhsT=codes[:, columns].bitcast(FP8X4), lhsT_scale=code_scales[:, columns],
+                                rhs=picked_words[h][:].bitcast(FP8X4), rhs_scale=picked_scales[h][:], start=True, stop=True)
             return bank[:].rearrange("p (v d) -> p d v", d=D)
 
-        def deal(raw, name, e, move):
-            grouped = tile([P, 2, P * PACK], BF16, f"{name}_bf{e}")
-            src = raw[:].rearrange("p j (m e t) -> p e m j t", e=2, t=2)
-            move(grouped[:].rearrange("p t (m j) -> p m j t", j=PACK), src[:, e])
-            codes = tile([P, 2 * P], U32, f"{name}_cd{e}")
-            scl = tile([P, 2 * P], U8, f"{name}_sc{e}")
-            nc.vector.quantize_mx(out=codes[:].bitcast(FP8X4), scales=scl[:], in_=grouped[:].rearrange("p t c -> p (t c)"))
-            return codes, scl
+        def branches(h):
+            return slice(h * BANK_BRANCHES, (h + 1) * BANK_BRANCHES)
 
-        w2_q = [deal(w2_raw, "w2", 0, nc.vector.tensor_copy), deal(w2_raw, "w2", 1, nc.scalar.copy)]
+        w2_mx = quantise_weights(w2_raw, "w2")
 
-        keep2 = [tile([P, 2, D, V], F32, f"keep{e}") for e in range(2)]
-        keepp = [keep2[t // 2][:, t % 2] for t in range(PACK)]
-        tree = [tile([P, 3, V], F32, f"tree{t}") for t in range(PACK)]
-        prod = [tile([P, 2, V], F32, f"prod{e}") for e in range(2)]
+        calm_pair = [tile([P, 2, D, V], F32, f"calm{e}") for e in range(2)]
+        calm = [calm_pair[t // 2][:, t % 2] for t in range(PACK)]
+        ent_sum = [tile([P, 3, V], F32, f"ent_sum{t}") for t in range(PACK)]
+        calm_product = [tile([P, 2, V], F32, f"calm_product{e}") for e in range(2)]
+
         en = {}
-        for t in range(PACK):
+        for t in range(2):
             for h in range(HALVES):
-                en[t, h] = product(w2_q, t, h)
-                nc.scalar.activation(keepp[t][:, :, h * VB : (h + 1) * VB], en[t, h], ACT.Sigmoid, scale=-1.0)
-        w1_q = [deal(w1_raw, "w1", 0, nc.vector.tensor_copy), deal(w1_raw, "w1", 1, nc.scalar.copy)]
-        for t2 in range(0, PACK, 2):
+                en[t, h] = product(w2_mx, t, h)
+                en[t + 2, h] = product(w2_mx, t + 2, h)
+
+        def make_calm(tiles):
+            for t in tiles:
+                for h in range(HALVES):
+                    nc.scalar.activation(calm[t][:, :, branches(h)], en[t, h], ACT.Sigmoid, scale=-1.0)
+
+        def make_excess(tiles):
             for d in range(D):
-                for t in (t2, t2 + 1):
+                for t in tiles:
                     for h in range(HALVES):
-                        ex = tree[t][:, 2, h * VB : (h + 1) * VB]
+                        excess = ent_sum[t][:, 2, branches(h)]
                         if d == 0:
-                            nc.vector.tensor_scalar(ex, en[t, h][:, d, :], KNEE, D * KNEE, ALU.max, ALU.subtract)
+                            nc.vector.tensor_scalar(excess, en[t, h][:, d, :], KNEE, D * KNEE, ALU.max, ALU.subtract)
                         else:
-                            nc.vector.scalar_tensor_tensor(ex, en[t, h][:, d, :], KNEE, ex, ALU.max, ALU.add)
-        for d in range(D):
-            for e in range(2):
-                if d == 0:
-                    nc.vector.tensor_scalar(prod[e][:], keep2[e][:, :, d, :], floor[:], None, ALU.max)
-                else:
-                    nc.vector.scalar_tensor_tensor(prod[e][:], keep2[e][:, :, d, :], floor[:], prod[e][:], ALU.max, ALU.mult)
+                            nc.vector.scalar_tensor_tensor(excess, en[t, h][:, d, :], KNEE, excess, ALU.max, ALU.add)
 
-        like = [tile([P, D, V], F32, f"like{t}") for t in range(PACK)]
+        make_excess((0, 1))
+        make_calm((2, 3))
+        make_calm((0, 1))
+        w1_mx = quantise_weights(w1_raw, "w1")
+        make_excess((2, 3))
+
+        for d in range(D):
+            for e in (1, 0):
+                plane = calm_pair[e][:, :, d, :]
+                if d == 0:
+                    nc.vector.tensor_scalar(calm_product[e][:], plane, floor[:], None, ALU.max)
+                else:
+                    nc.vector.scalar_tensor_tensor(calm_product[e][:], plane, floor[:], calm_product[e][:], ALU.max, ALU.mult)
+
+        likely = [tile([P, D, V], F32, f"likely{t}") for t in range(PACK)]
         for t in range(PACK):
             for h in range(HALVES):
-                lg = product(w1_q, t, h)
-                nc.scalar.activation(like[t][:, :, h * VB : (h + 1) * VB], lg, ACT.Sigmoid)
-
+                nc.scalar.activation(likely[t][:, :, branches(h)], product(w1_mx, t, h), ACT.Sigmoid)
 
         for t in range(PACK):
-            nc.scalar.activation(tree[t][:, 1, :], prod[t // 2][:, t % 2, :], ACT.Ln, scale=LIFT)
+            nc.scalar.activation(ent_sum[t][:, 1, :], calm_product[t // 2][:, t % 2, :], ACT.Ln, scale=LIFT)
 
-        quarter = tile([P, PACK], F32, "quarter")
-        nc.vector.tensor_scalar(quarter[:], unit_sb[:], 1.0 / D, None, ALU.mult)
+        unit_mean = tile([P, PACK], F32, "unit_mean")
+        nc.vector.tensor_scalar(unit_mean[:], unit_sb[:], 1.0 / D, None, ALU.mult)
 
         gain = [tile([P, 3, V], F32, f"gain{t}") for t in range(PACK)]
-        gb = [tile([P, PACK, RW], F32, f"gb{r}") for r in range(RH)]
-        tb = [tile([P, U], F32, f"tb{t}") for t in range(PACK)]
+        gain_picked = [tile([P, PACK, GAIN_WIDTH], F32, f"gain_picked{r}") for r in range(U // GAIN_WIDTH)]
+        ent_picked = [tile([P, U], F32, f"ent_picked{t}") for t in range(PACK)]
 
-        bcols = RW // 16
+        def window(rows):
+            return rows[:].rearrange("p a v -> p (a v)")
 
-        def window(tl):
-            return tl[:].rearrange("p a v -> p (a v)")
-
-        def make_gain(tiles):
-            both = keep.tile([P, 2, 2, V], F32, name=f"side{tiles[0]}", tag=f"shared{tiles[0]}", align_bytes=64)
-            side = {t: both[:, t % 2] for t in tiles}
+        def make_gain(tiles, tag):
+            pair = sbuf.tile([P, 2, 2, V], F32, name=f"even_sums{tiles[0]}", tag=tag, align_bytes=64)
+            even_sums = {t: pair[:, t % 2] for t in tiles}
             for t in tiles:
-                nc.vector.tensor_tensor(acc[t][:, :, 0:V], keepp[t], like[t][:], ALU.mult)
+                nc.vector.tensor_tensor(acc[t][:, :, 0:V], calm[t], likely[t][:], ALU.mult)
             for t in tiles:
-                nc.vector.tensor_tensor(side[t][:, 0, :], acc[t][:, 0, 0:V], acc[t][:, 2, 0:V], ALU.add)
+                nc.vector.tensor_tensor(even_sums[t][:, 0, :], acc[t][:, 0, 0:V], acc[t][:, 2, 0:V], ALU.add)
             for t in tiles:
-                nc.vector.tensor_tensor(side[t][:, 1, :], acc[t][:, 2, 0:V], acc[t][:, 0, 1 : V + 1], ALU.add)
+                nc.vector.tensor_tensor(even_sums[t][:, 1, :], acc[t][:, 2, 0:V], acc[t][:, 0, 1 : V + 1], ALU.add)
             for t in tiles:
-                nc.vector.scalar_tensor_tensor(gain[t][:, 1:3, :], side[t], unit_sb[:, t : t + 1], acc[t][:, 1:4:2, 0:V], ALU.mult, ALU.mult)
+                nc.vector.scalar_tensor_tensor(gain[t][:, 1:3, :], even_sums[t], unit_sb[:, t : t + 1], acc[t][:, 1:D:2, 0:V], ALU.mult, ALU.mult)
             for t in tiles:
                 nc.vector.tensor_tensor(gain[t][:, 0, :], gain[t][:, 1, :], gain[t][:, 2, :], ALU.add)
-
-        def fetch(dst, src, tiles):
-            for r in range(RH):
+            for r in range(U // GAIN_WIDTH):
+                offsets = bud_sb[:, r * GAIN_WIDTH // PER_COLUMN : (r + 1) * GAIN_WIDTH // PER_COLUMN]
                 for t in tiles:
-                    nc.scalar.activation(dst[r][:, t, :], window(src[t]).indirect(bud_sb[:, r * bcols : (r + 1) * bcols]), ACT.Copy)
+                    nc.scalar.activation(gain_picked[r][:, t, :], window(gain[t]).indirect(offsets), ACT.Copy)
 
         for t in range(PACK):
-            nc.vector.scalar_tensor_tensor(tree[t][:, 0, :], tree[t][:, 2, :], math.log(LIFT), tree[t][:, 1, :], ALU.add, ALU.subtract)
+            nc.vector.scalar_tensor_tensor(ent_sum[t][:, 0, :], ent_sum[t][:, 2, :], math.log(LIFT), ent_sum[t][:, 1, :], ALU.add, ALU.subtract)
         for t in range(PACK):
-            nc.scalar.activation(tb[t][:], window(tree[t]).indirect(bud_sb[:]), ACT.Copy)
-        make_gain((0, 1))
-        fetch(gb, gain, (0, 1))
-        w3_bf = tile([P, N, PACK], BF16, "w3_bf")
-        nc.scalar.copy(w3_bf[:], w3_raw[:].rearrange("p j c -> p c j"))
-        w3_cd = tile([P, N], U32, "w3_cd")
-        w3_sc = tile([P, N], U8, "w3_sc")
-        nc.vector.quantize_mx(out=w3_cd[:].bitcast(FP8X4), scales=w3_sc[:], in_=w3_bf[:].rearrange("p c j -> p (c j)"))
-        make_gain((2, 3))
-        fetch(gb, gain, (2, 3))
-        spent = keep.tile([P, PACK, U], F32, name="spent", tag="shared2", align_bytes=64)
+            nc.scalar.activation(ent_picked[t][:], window(ent_sum[t]).indirect(bud_sb[:]), ACT.Copy)
+        make_gain((0, 1), "first_sums")
+
+        w3_rounded = tile([P, N, PACK], BF16, "w3_rounded")
+        nc.scalar.copy(w3_rounded[:], w3_raw[:].rearrange("p j c -> p c j"))
+        w3_codes = tile([P, N], U32, "w3_codes")
+        w3_scales = tile([P, N], U8, "w3_scales")
+        nc.vector.quantize_mx(out=w3_codes[:].bitcast(FP8X4), scales=w3_scales[:], in_=w3_rounded[:].rearrange("p c j -> p (c j)"))
+
+        make_gain((2, 3), "second_sums")
+        spent = sbuf.tile([P, PACK, U], F32, name="spent", tag="second_sums", align_bytes=64)
         for t in range(PACK):
-            nc.vector.scalar_tensor_tensor(spent[:, t, :], tb[t][:], quarter[:, t : t + 1], cost_sb[:, t, :], ALU.mult, ALU.mult)
+            nc.vector.scalar_tensor_tensor(spent[:, t, :], ent_picked[t][:], unit_mean[:, t : t + 1], cost_sb[:, t, :], ALU.mult, ALU.mult)
 
-        CW = 128
-        pieces = U // CW
-        per = RW // CW
-        hid = [tile([P, CW, PACK], BF16, f"hid{c}") for c in range(pieces)]
+        pieces = U // PIECE
+        hid = [tile([P, PIECE, PACK], BF16, f"hid{c}") for c in range(pieces)]
 
-        flat = [tile([P, PACK, CW], BF16, f"flat{c}") for c in range(pieces)]
-
-        def subtract(c):
-            cols_c = slice((c % per) * CW, (c % per + 1) * CW)
-            nc.vector.tensor_tensor(flat[c][:], gb[c // per][:, :, cols_c], spent[:, :, c * CW : (c + 1) * CW], ALU.subtract)
-
-        def weave(c):
-            move = nc.vector.tensor_copy if c == pieces - 1 else nc.scalar.copy
-            move(hid[c][:], flat[c][:].rearrange("p t c -> p c t"))
+        def make_hid(c):
+            r, start = divmod(c * PIECE, GAIN_WIDTH)
+            nc.vector.tensor_tensor(hid[c][:].rearrange("p (c i) t -> p c t i", i=4),
+                                    gain_picked[r][:, :, start : start + PIECE].rearrange("p t (c i) -> p c t i", i=4),
+                                    spent[:, :, c * PIECE : (c + 1) * PIECE].rearrange("p t (c i) -> p c t i", i=4), ALU.subtract)
 
         def finish(c):
-            h_cd = tile([P, CW], U32, f"h_cd{c}")
-            h_sc = tile([P, CW], U8, f"h_sc{c}")
-            nc.vector.quantize_mx(out=h_cd[:].bitcast(FP8X4), scales=h_sc[:], in_=hid[c][:].rearrange("p c t -> p (c t)"))
+            hid_codes = tile([P, PIECE], U32, f"hid_codes{c}")
+            hid_scales = tile([P, PIECE], U8, f"hid_scales{c}")
+            nc.vector.quantize_mx(out=hid_codes[:].bitcast(FP8X4), scales=hid_scales[:], in_=hid[c][:].rearrange("p r t -> p (r t)"))
             bank = psum.tile([P, BANK], F32, name="bank")
             for m in range(N // P):
-                nc.tensor.matmul_mx(out=bank[:, m * CW : (m + 1) * CW], lhsT=w3_cd[:, m * P : (m + 1) * P].bitcast(FP8X4),
-                                    lhsT_scale=w3_sc[:, m * P : (m + 1) * P], rhs=h_cd[:].bitcast(FP8X4), rhs_scale=h_sc[:],
-                                    start=True, stop=True)
-            res = tile([P, N // P, CW], F32, f"res{c}")
-            nc.scalar.copy(res[:].rearrange("p m c -> p (m c)"), bank[:, 0 : (N // P) * CW])
-            nc.sync.dma_start(out[:, c * CW : (c + 1) * CW].rearrange("(m p) c -> p m c", p=P), res[:])
+                nc.tensor.matmul_mx(out=bank[:, m * PIECE : (m + 1) * PIECE], lhsT=w3_codes[:, m * P : (m + 1) * P].bitcast(FP8X4),
+                                    lhsT_scale=w3_scales[:, m * P : (m + 1) * P], rhs=hid_codes[:].bitcast(FP8X4),
+                                    rhs_scale=hid_scales[:], start=True, stop=True)
+            result = tile([P, N // P, PIECE], F32, f"result{c}")
+            copy = nc.vector.tensor_copy if c == pieces - 1 else nc.scalar.copy
+            copy(result[:].rearrange("p m r -> p (m r)"), bank[:, 0 : (N // P) * PIECE])
+            nc.sync.dma_start(out[:, c * PIECE : (c + 1) * PIECE].rearrange("(m p) r -> p m r", p=P), result[:])
 
-        for step in range(pieces + 2):
+        for step in range(pieces + 1):
             if step < pieces:
-                subtract(step)
-            if 1 <= step <= pieces:
-                weave(step - 1)
-            if step >= 2:
-                finish(step - 2)
+                make_hid(step)
+            if step >= 1:
+                finish(step - 1)

from contextlib import ExitStack
import math

import concourse.mybir as mybir

K, T, S, D, N, H, V, U = 512, 2048, 1024, 4, 256, 512, 256, 512
FLOPS = 2 * K * H * S * 2 + 2 * H * N * U

F32 = mybir.dt.float32
BF16 = mybir.dt.bfloat16
I32 = mybir.dt.int32
U32 = mybir.dt.uint32
U16 = mybir.dt.uint16
U8 = mybir.dt.uint8
FP8X4 = mybir.dt.float8_e4m3fn_x4
ACT = mybir.ActivationFunctionType
ALU = mybir.AluOpType

P = 128
PACK = 4
PER_COLUMN = 16
BANK = 512
HALVES = S // BANK
BANK_BRANCHES = BANK // D
PITCH = V + 8
KNEE = 12.25
LIFT = 256.0
GAIN_WIDTH = 256
PIECE = 128


def tile_picked_yentrd_net_p_kernel(tc, x_words, x_scales, w1, w2, cost, unit, w3, offs, bud, out):
    nc = tc.nc
    with ExitStack() as ctx:
        sbuf = ctx.enter_context(tc.tile_pool(name="sbuf", bufs=1))
        psum = ctx.enter_context(tc.psum_pool(name="psum", bufs=8))

        def tile(shape, dtype, name):
            return sbuf.tile(shape, dtype, name=name, align_bytes=64)

        offs_sb = tile([P, S // PER_COLUMN], U16, "offs_sb")
        bud_sb = tile([P, U // PER_COLUMN], U16, "bud_sb")
        words = tile([P, T], U32, "words")
        scales = tile([P, T], U8, "scales")
        w2_raw = tile([P, PACK, H], F32, "w2_raw")
        w1_raw = tile([P, PACK, H], F32, "w1_raw")
        w3_raw = tile([P, PACK, N], F32, "w3_raw")
        cost_sb = tile([P, PACK, U], F32, "cost_sb")
        unit_sb = tile([P, PACK], F32, "unit_sb")

        nc.sync.dma_start(offs_sb[:], offs)
        for q in range(4):
            rows = x_scales[0, 4 * q : 4 * q + 4, :].bitcast(I32)
            nc.sync.dma_start(scales[32 * q : 32 * q + 32, :].bitcast(I32), rows.partition_broadcast(8))
        nc.sync.dma_start(words[:].bitcast(I32), x_words[0].rearrange("p n b -> p (n b)").bitcast(I32))
        nc.sync.dma_start(w2_raw[:], w2.rearrange("(p j) c -> p j c", j=PACK))
        nc.sync.dma_start(w3_raw[:], w3.rearrange("(p j) c -> p j c", j=PACK))
        nc.sync.dma_start(w1_raw[:], w1.rearrange("(p j) c -> p j c", j=PACK))
        nc.sync.dma_start(bud_sb[:], bud)
        nc.sync.dma_start(unit_sb[:], unit.rearrange("(p t) o -> p (t o)", t=PACK))
        nc.sync.dma_start(cost_sb[:], cost.rearrange("(p t) r -> p t r", t=PACK))

        knee = tile([P, 1], F32, "knee")
        nc.gpsimd.memset(knee[:], KNEE)
        floor = tile([P, 1], F32, "floor")
        nc.scalar.activation(floor[:], knee[:], ACT.Sigmoid, scale=-1.0)
        acc = [tile([P, D, PITCH], F32, f"acc{t}") for t in range(PACK)]
        for t in range(PACK):
            nc.gpsimd.memset(acc[t][:, 0, V : V + 1], 0.0)

        picked_scales = [tile([P, BANK], U8, f"picked_scales{h}") for h in range(HALVES)]
        picked_words = [tile([P, BANK], U32, f"picked_words{h}") for h in range(HALVES)]
        offs_half = [offs_sb[:, h * BANK // PER_COLUMN : (h + 1) * BANK // PER_COLUMN] for h in range(HALVES)]
        for h in range(HALVES):
            nc.vector.tensor_copy(picked_scales[h][:], scales[:].indirect(offs_half[h]))
        for h in range(HALVES):
            nc.vector.tensor_copy(picked_words[h][:], words[:].indirect(offs_half[h]))

        def quantise_pair(raw, name, e, copy):
            rounded = tile([P, 2, P * PACK], BF16, f"{name}_rounded{e}")
            source = raw[:].rearrange("p j (m e s) -> p e m j s", e=2, s=2)
            copy(rounded[:].rearrange("p s (m j) -> p m j s", j=PACK), source[:, e])
            codes = tile([P, 2 * P], U32, f"{name}_codes{e}")
            code_scales = tile([P, 2 * P], U8, f"{name}_scales{e}")
            nc.vector.quantize_mx(out=codes[:].bitcast(FP8X4), scales=code_scales[:], in_=rounded[:].rearrange("p s c -> p (s c)"))
            return codes, code_scales

        def quantise_weights(raw, name):
            return [quantise_pair(raw, name, 0, nc.vector.tensor_copy), quantise_pair(raw, name, 1, nc.scalar.copy)]

        def product(weights, t, h):
            codes, code_scales = weights[t // 2]
            columns = slice((t % 2) * P, (t % 2 + 1) * P)
            bank = psum.tile([P, BANK], F32, name="bank")
            nc.tensor.matmul_mx(out=bank[:], lhsT=codes[:, columns].bitcast(FP8X4), lhsT_scale=code_scales[:, columns],
                                rhs=picked_words[h][:].bitcast(FP8X4), rhs_scale=picked_scales[h][:], start=True, stop=True)
            return bank[:].rearrange("p (v d) -> p d v", d=D)

        def branches(h):
            return slice(h * BANK_BRANCHES, (h + 1) * BANK_BRANCHES)

        w2_mx = quantise_weights(w2_raw, "w2")

        calm_pair = [tile([P, 2, D, V], F32, f"calm{e}") for e in range(2)]
        calm = [calm_pair[t // 2][:, t % 2] for t in range(PACK)]
        ent_sum = [tile([P, 3, V], F32, f"ent_sum{t}") for t in range(PACK)]
        calm_product = [tile([P, 2, V], F32, f"calm_product{e}") for e in range(2)]

        en = {}
        for t in range(2):
            for h in range(HALVES):
                en[t, h] = product(w2_mx, t, h)
                en[t + 2, h] = product(w2_mx, t + 2, h)

        def make_calm(tiles):
            for t in tiles:
                for h in range(HALVES):
                    nc.scalar.activation(calm[t][:, :, branches(h)], en[t, h], ACT.Sigmoid, scale=-1.0)

        def make_excess(tiles):
            for d in range(D):
                for t in tiles:
                    for h in range(HALVES):
                        excess = ent_sum[t][:, 2, branches(h)]
                        if d == 0:
                            nc.vector.tensor_scalar(excess, en[t, h][:, d, :], KNEE, D * KNEE, ALU.max, ALU.subtract)
                        else:
                            nc.vector.scalar_tensor_tensor(excess, en[t, h][:, d, :], KNEE, excess, ALU.max, ALU.add)

        make_excess((0, 1))
        make_calm((2, 3))
        make_calm((0, 1))
        w1_mx = quantise_weights(w1_raw, "w1")
        make_excess((2, 3))

        for d in range(D):
            for e in (1, 0):
                plane = calm_pair[e][:, :, d, :]
                if d == 0:
                    nc.vector.tensor_scalar(calm_product[e][:], plane, floor[:], None, ALU.max)
                else:
                    nc.vector.scalar_tensor_tensor(calm_product[e][:], plane, floor[:], calm_product[e][:], ALU.max, ALU.mult)

        likely = [tile([P, D, V], F32, f"likely{t}") for t in range(PACK)]
        for t in range(PACK):
            for h in range(HALVES):
                nc.scalar.activation(likely[t][:, :, branches(h)], product(w1_mx, t, h), ACT.Sigmoid)

        for t in range(PACK):
            nc.scalar.activation(ent_sum[t][:, 1, :], calm_product[t // 2][:, t % 2, :], ACT.Ln, scale=LIFT)

        unit_mean = tile([P, PACK], F32, "unit_mean")
        nc.vector.tensor_scalar(unit_mean[:], unit_sb[:], 1.0 / D, None, ALU.mult)

        gain = [tile([P, 3, V], F32, f"gain{t}") for t in range(PACK)]
        gain_picked = [tile([P, PACK, GAIN_WIDTH], F32, f"gain_picked{r}") for r in range(U // GAIN_WIDTH)]
        ent_picked = [tile([P, U], F32, f"ent_picked{t}") for t in range(PACK)]

        def window(rows):
            return rows[:].rearrange("p a v -> p (a v)")

        def make_gain(tiles, tag):
            pair = sbuf.tile([P, 2, 2, V], F32, name=f"even_sums{tiles[0]}", tag=tag, align_bytes=64)
            even_sums = {t: pair[:, t % 2] for t in tiles}
            for t in tiles:
                nc.vector.tensor_tensor(acc[t][:, :, 0:V], calm[t], likely[t][:], ALU.mult)
            for t in tiles:
                nc.vector.tensor_tensor(even_sums[t][:, 0, :], acc[t][:, 0, 0:V], acc[t][:, 2, 0:V], ALU.add)
            for t in tiles:
                nc.vector.tensor_tensor(even_sums[t][:, 1, :], acc[t][:, 2, 0:V], acc[t][:, 0, 1 : V + 1], ALU.add)
            for t in tiles:
                nc.vector.scalar_tensor_tensor(gain[t][:, 1:3, :], even_sums[t], unit_sb[:, t : t + 1], acc[t][:, 1:D:2, 0:V], ALU.mult, ALU.mult)
            for t in tiles:
                nc.vector.tensor_tensor(gain[t][:, 0, :], gain[t][:, 1, :], gain[t][:, 2, :], ALU.add)
            for r in range(U // GAIN_WIDTH):
                offsets = bud_sb[:, r * GAIN_WIDTH // PER_COLUMN : (r + 1) * GAIN_WIDTH // PER_COLUMN]
                for t in tiles:
                    nc.scalar.activation(gain_picked[r][:, t, :], window(gain[t]).indirect(offsets), ACT.Copy)

        for t in range(PACK):
            nc.vector.scalar_tensor_tensor(ent_sum[t][:, 0, :], ent_sum[t][:, 2, :], math.log(LIFT), ent_sum[t][:, 1, :], ALU.add, ALU.subtract)
        for t in range(PACK):
            nc.scalar.activation(ent_picked[t][:], window(ent_sum[t]).indirect(bud_sb[:]), ACT.Copy)
        make_gain((0, 1), "first_sums")

        w3_rounded = tile([P, N, PACK], BF16, "w3_rounded")
        nc.scalar.copy(w3_rounded[:], w3_raw[:].rearrange("p j c -> p c j"))
        w3_codes = tile([P, N], U32, "w3_codes")
        w3_scales = tile([P, N], U8, "w3_scales")
        nc.vector.quantize_mx(out=w3_codes[:].bitcast(FP8X4), scales=w3_scales[:], in_=w3_rounded[:].rearrange("p c j -> p (c j)"))

        make_gain((2, 3), "second_sums")
        spent = sbuf.tile([P, PACK, U], F32, name="spent", tag="second_sums", align_bytes=64)
        for t in range(PACK):
            nc.vector.scalar_tensor_tensor(spent[:, t, :], ent_picked[t][:], unit_mean[:, t : t + 1], cost_sb[:, t, :], ALU.mult, ALU.mult)

        pieces = U // PIECE
        hid = [tile([P, PIECE, PACK], BF16, f"hid{c}") for c in range(pieces)]

        def make_hid(c):
            r, start = divmod(c * PIECE, GAIN_WIDTH)
            nc.vector.tensor_tensor(hid[c][:].rearrange("p (c i) t -> p c t i", i=4),
                                    gain_picked[r][:, :, start : start + PIECE].rearrange("p t (c i) -> p c t i", i=4),
                                    spent[:, :, c * PIECE : (c + 1) * PIECE].rearrange("p t (c i) -> p c t i", i=4), ALU.subtract)

        def finish(c):
            hid_codes = tile([P, PIECE], U32, f"hid_codes{c}")
            hid_scales = tile([P, PIECE], U8, f"hid_scales{c}")
            nc.vector.quantize_mx(out=hid_codes[:].bitcast(FP8X4), scales=hid_scales[:], in_=hid[c][:].rearrange("p r t -> p (r t)"))
            bank = psum.tile([P, BANK], F32, name="bank")
            for m in range(N // P):
                nc.tensor.matmul_mx(out=bank[:, m * PIECE : (m + 1) * PIECE], lhsT=w3_codes[:, m * P : (m + 1) * P].bitcast(FP8X4),
                                    lhsT_scale=w3_scales[:, m * P : (m + 1) * P], rhs=hid_codes[:].bitcast(FP8X4),
                                    rhs_scale=hid_scales[:], start=True, stop=True)
            result = tile([P, N // P, PIECE], F32, f"result{c}")
            copy = nc.vector.tensor_copy if c == pieces - 1 else nc.scalar.copy
            copy(result[:].rearrange("p m r -> p (m r)"), bank[:, 0 : (N // P) * PIECE])
            nc.sync.dma_start(out[:, c * PIECE : (c + 1) * PIECE].rearrange("(m p) r -> p m r", p=P), result[:])

        for step in range(pieces + 1):
            if step < pieces:
                make_hid(step)
            if step >= 1:
                finish(step - 1)
